import numpy as np
import ml_dtypes


def mxq(x, axis, fmt="e4m3"):
    dtype, down = {"e4m3": (ml_dtypes.float8_e4m3fn, 7), "e5m2": (ml_dtypes.float8_e5m2, 14)}[fmt]
    v = np.moveaxis(np.asarray(x, np.float32).astype(ml_dtypes.bfloat16).astype(np.float64), axis, -1)
    blocks = v.reshape(v.shape[:-1] + (-1, 32))
    amax = np.abs(blocks).max(-1, keepdims=True)
    byte = np.maximum(np.where(amax > 0, np.frexp(amax)[1] - 1 + 127, 0) - down, 1)
    scale = np.exp2(byte - 127.0)
    codes = (blocks / scale).astype(np.float32).astype(dtype).astype(np.float64)
    return np.moveaxis((codes * scale).reshape(v.shape), -1, axis)


WIDE = False


def mx_kscale(k):
    if not WIDE:
        return np.ones(k)
    levels = np.array([10, -10, 5, -5, 0])
    if k % 512:
        return np.exp2(np.random.permutation(np.resize(levels, k // 32))).repeat(32)
    a = np.empty((k // 512, 16))
    for p in range(k // 512):
        a[p, :8] = np.random.permutation(np.resize(levels, 8))
        for g in range(8):
            far = levels[np.abs(levels - a[p, g]) >= 10]
            a[p, g + 8] = far[np.random.randint(len(far))]
    return np.exp2(a.ravel()).repeat(32)


def f64(x):
    return np.asarray(x).astype(np.float64)


def striped(idx):
    return np.tile(idx.reshape(-1, 16).T, (8, 1)).astype(np.uint16)


def unstriped(offs):
    return offs[:16].T.reshape(-1).astype(np.int64)


def pack_weight(w):
    k, n = w.shape
    w = f64(np.asarray(w, np.float32).astype(ml_dtypes.bfloat16)).reshape(k // 32, 32, n)
    amax = np.abs(w).max(1)
    byte = np.clip(np.where(amax > 0, np.frexp(amax)[1] - 1 + 127 - 7, 1), 1, 254)
    scaled = (w * np.exp2(127.0 - byte)[:, None, :]).reshape(k, n).astype(np.float32)
    words = np.ascontiguousarray(scaled.reshape(k // 512, 128, 4, n).transpose(0, 1, 3, 2)).astype(ml_dtypes.float8_e4m3fn).view(np.uint8)
    return words, np.ascontiguousarray(byte.astype(np.uint8).reshape(k // 512, 16, n))


def unpack_weight(words, scales):
    g, p, n, _ = words.shape
    vals = np.ascontiguousarray(words).view(ml_dtypes.float8_e4m3fn).astype(np.float64) * np.repeat(np.exp2(scales.astype(np.float64) - 127.0), 8, axis=1)[..., None]
    return vals.transpose(0, 1, 3, 2).reshape(g * 512, n)


E2M1 = np.array([0.0, 0.5, 1.0, 1.5, 2.0, 3.0, 4.0, 6.0, -0.0, -0.5, -1.0, -1.5, -2.0, -3.0, -4.0, -6.0])


def pack_fp4(w):
    k, n = w.shape
    w = f64(np.asarray(w, np.float32).astype(ml_dtypes.bfloat16)).reshape(k // 32, 32, n)
    amax = np.abs(w).max(1)
    mant, ex = np.frexp(amax / 6.0)
    byte = np.clip(np.where(amax > 0, np.where(mant > 0.5, ex, ex - 1) + 127, 1), 1, 254)
    scaled = (w * np.exp2(127.0 - byte)[:, None, :]).reshape(k, n).astype(np.float32)
    c = np.ascontiguousarray(scaled.reshape(k // 512, 128, 4, n).transpose(0, 1, 3, 2)).astype(ml_dtypes.float4_e2m1fn).view(np.uint8) & 0xF
    words = (c[..., 0::2] | (c[..., 1::2] << 4)).reshape(k // 512, 128, 2 * n)
    return np.ascontiguousarray(words), np.ascontiguousarray(byte.astype(np.uint8).reshape(k // 512, 16, n))


def unpack_fp4(words, scales):
    g, _, n = scales.shape
    words = np.ascontiguousarray(words).reshape(g, 128, n, 2)
    nib = np.empty((g, 128, n, 4), np.uint8)
    nib[..., 0::2] = words & 0xF
    nib[..., 1::2] = words >> 4
    vals = E2M1[nib] * np.repeat(np.exp2(scales.astype(np.float64) - 127.0), 8, axis=1)[..., None]
    return vals.transpose(0, 1, 3, 2).reshape(g * 512, n)


def sigmoid(v):
    return 1.0 / (1.0 + np.exp(-np.maximum(v, -700.0)))


K, T, S, N, H = 1024, 1024, 512, 256, 512


def setup_inputs():
    n = np.random.standard_normal
    s = mx_kscale(K)[:, None]
    u = mx_kscale(H)
    packed_xT = pack_weight(n((K, T)) * s)
    packed_w1 = pack_fp4(n((K, H)) / np.sqrt(K) / s)
    packed_w2 = pack_fp4(n((K, H)) / np.sqrt(K) / s)
    packed_w3 = pack_fp4(n((K, H)) / np.sqrt(K) / s)
    packed_w4 = pack_fp4(n((H, N)) / np.sqrt(H) / u[:, None])
    return {
        "x_words": packed_xT[0],
        "x_scales": packed_xT[1],
        "w1_words": packed_w1[0],
        "w1_scales": packed_w1[1],
        "w2_words": packed_w2[0],
        "w2_scales": packed_w2[1],
        "w3_words": packed_w3[0],
        "w3_scales": packed_w3[1],
        "trt": (np.random.uniform(0.0, 1.0, (H, S))).astype(np.float32),
        "yy0": (n((H, S))).astype(np.float32),
        "unit": (np.random.uniform(0.6, 1.4, (H, 1)) * u[:, None]).astype(np.float32),
        "w4_words": packed_w4[0],
        "w4_scales": packed_w4[1],
        "offs": striped(np.random.permutation(T)[:S]),
        "tw": striped(np.random.permutation(S)),
    }


def reference(x_words, x_scales, w1_words, w1_scales, w2_words, w2_scales, w3_words, w3_scales, trt, yy0, unit, w4_words, w4_scales, offs, tw):
    xq = unpack_weight(x_words, x_scales)[:, unstriped(offs)]
    m1 = unpack_fp4(w2_words, w2_scales).T @ xq
    m0 = unpack_fp4(w1_words, w1_scales).T @ xq
    pe = unpack_fp4(w3_words, w3_scales).T @ xq
    prop = 0.8 * sigmoid(pe) + 0.1
    clev = (f64(trt) - prop) / (prop * (-1.0 * prop + 1.0))
    resid = f64(yy0) - (f64(trt) * m1 + (-1.0 * f64(trt) + 1.0) * m0)
    tau = m1 - m0 + 0.3 * (clev * resid)
    tt = tau[:, unstriped(tw)]
    hid = f64(unit) * (tau * (prop / (np.abs(tt) + 0.6)))
    return unpack_fp4(w4_words, w4_scales).T @ mxq(hid, 0, "e4m3")

@@ -1,0 +1,289 @@
+import math
+from contextlib import ExitStack
+
+import concourse.mybir as mybir
+from concourse.masks import make_identity
+
+K, T, S, N, H = 1024, 1024, 512, 256, 512
+FLOPS = 2 * (3 * K * H * S + H * N * S)
+
+F32 = mybir.dt.float32
+BF16 = mybir.dt.bfloat16
+I32 = mybir.dt.int32
+U32 = mybir.dt.uint32
+U16 = mybir.dt.uint16
+U8 = mybir.dt.uint8
+FP8X4 = mybir.dt.float8_e4m3fn_x4
+FP4X4 = mybir.dt.float4_e2m1fn_x4
+ALU = mybir.AluOpType
+ACT = mybir.ActivationFunctionType
+
+P = 128
+PACK = 4
+PASSES = K // (P * PACK)
+JT = S // P
+HALF = S // 2
+HALF_LN9 = 0.5 * math.log(9.0)
+
+
+def tile_picked_yuplif_rel_p_kernel(
+    tc, x_words, x_scales, w1_words, w1_scales, w2_words, w2_scales, w3_words, w3_scales,
+    trt, yy0, unit, w4_words, w4_scales, offs, tw, out,
+):
+    nc = tc.nc
+    with ExitStack() as ctx:
+        keep = ctx.enter_context(tc.tile_pool(name="keep", bufs=1))
+        psum = ctx.enter_context(tc.psum_pool(name="psum", bufs=1))
+
+        def sb(name, shape, dtype=F32):
+            return keep.tile(shape, dtype, name=name, tag=name, align_bytes=64)
+
+        def bank(tag, shape, name):
+            return psum.tile(shape, F32, name=name, tag=tag)
+
+        def load_scales(queue, tile, scales, quadrants):
+            for q in quadrants:
+                queue.dma_start(
+                    out=tile[32 * q : 32 * q + 4, :, :].bitcast(I32),
+                    in_=scales[:, 4 * q : 4 * q + 4, :].rearrange("o r c -> r o c").bitcast(I32),
+                )
+
+        def load_fp4(queue, tile, words):
+            queue.dma_start(out=tile[:].bitcast(I32), in_=words.rearrange("o p c -> p o c").bitcast(I32))
+
+        offs_sb = keep.tile([P, S // 16], U16, name="offs_sb")
+        tw_sb = keep.tile([P, S // 16], U16, name="tw_sb")
+        xw = [sb("xw%d" % o, [P, T], U32) for o in range(PASSES)]
+        xs = sb("xs", [P, PASSES, T], U8)
+        ww = [sb("ww%d" % a, [P, PASSES, 2 * H], U8) for a in range(3)]
+        ws = [sb("ws%d" % a, [P, PASSES, H], U8) for a in range(3)]
+        w4w = sb("w4w", [P, 1, 2 * N], U8)
+        w4s = sb("w4s", [P, 1, N], U8)
+        unit_sb = sb("unit_sb", [P, PACK])
+        unit4 = sb("unit4", [P, PACK])
+        trt_sb = [sb("trt%d" % h, [P, PACK, HALF]) for h in range(2)]
+        yy_sb = [sb("yy%d" % h, [P, PACK, HALF]) for h in range(2)]
+        ident = sb("ident", [P, P])
+
+        trt_v = trt.rearrange("(p t) j -> p t j", t=PACK)
+        yy_v = yy0.rearrange("(p t) j -> p t j", t=PACK)
+
+        def load_words(queue, o):
+            queue.dma_start(out=xw[o][:].bitcast(I32), in_=x_words[o].rearrange("p n t -> p (n t)").bitcast(I32))
+
+        nc.vector.memset(xs[:].rearrange("p o c -> p (o c)").bitcast(I32), 0)
+        load_scales(nc.gpsimd, ws[0], w1_scales, (0, 1, 2, 3))
+        make_identity(nc, ident[:])
+        nc.sync.dma_start(offs_sb[:], offs)
+        load_scales(nc.sync, xs, x_scales, (0, 1, 2, 3))
+        load_words(nc.scalar, 0)
+        load_words(nc.scalar, 1)
+        load_fp4(nc.scalar, ww[0], w1_words)
+        load_fp4(nc.scalar, ww[1], w2_words)
+        load_fp4(nc.scalar, ww[2], w3_words)
+        nc.scalar.dma_start(out=trt_sb[0][:], in_=trt_v[:, :, 0:HALF])
+        load_scales(nc.sync, ws[1], w2_scales, (0, 1, 2, 3))
+        load_scales(nc.sync, ws[2], w3_scales, (0, 1, 2, 3))
+        nc.sync.dma_start(out=yy_sb[0][:], in_=yy_v[:, :, 0:HALF])
+        nc.sync.dma_start(out=trt_sb[1][:], in_=trt_v[:, :, HALF:S])
+        nc.sync.dma_start(out=yy_sb[1][:], in_=yy_v[:, :, HALF:S])
+        nc.sync.dma_start(out=unit_sb[:], in_=unit.rearrange("(p t) o -> p (t o)", t=PACK))
+        nc.sync.dma_start(tw_sb[:], tw)
+        load_fp4(nc.sync, w4w, w4_words)
+        load_scales(nc.sync, w4s, w4_scales, (0, 1, 2, 3))
+
+        gw = [sb("gw%d" % o, [P, S], U32) for o in range(PASSES)]
+        gs = [sb("gs%d" % o, [P, S], U8) for o in range(PASSES)]
+
+        def pick_words(o, lo, hi):
+            nc.vector.tensor_copy(gw[o][:, lo:hi], xw[o][:].indirect(offs_sb[:, lo // 16 : hi // 16]))
+
+        def pick_scales(lo, hi):
+            for o in range(PASSES):
+                nc.vector.tensor_copy(gs[o][:, lo:hi], xs[:, o, :].indirect(offs_sb[:, lo // 16 : hi // 16]))
+
+        pick_words(0, 0, S)
+        pick_words(1, 0, S)
+        pick_scales(0, P)
+        pick_scales(P, S)
+
+        def product(j, a, tag):
+            acc = bank(tag, [P, H], "acc%d_%d" % (a, j))
+            for o in range(PASSES):
+                nc.tensor.matmul_mx(
+                    out=acc[:],
+                    lhsT=gw[o][:, j * P : (j + 1) * P].bitcast(FP8X4),
+                    lhsT_scale=gs[o][:, j * P : (j + 1) * P],
+                    rhs=ww[a][:, o, :].bitcast(FP4X4),
+                    rhs_scale=ws[a][:, o, :],
+                    start=(o == 0),
+                    stop=(o == PASSES - 1),
+                )
+            return acc[:].rearrange("p (m t) -> p t m", t=PACK)
+
+        def turned_sum(dst, terms):
+            for n, term in enumerate(terms):
+                nc.tensor.matmul(dst, term, ident[:], start=(n == 0), stop=(n == len(terms) - 1), is_transpose=True)
+
+        def turn(tag, name, tiles):
+            dst = bank(tag, [P, PACK, P], name)
+            for t in range(PACK):
+                turned_sum(dst[:, t, :], [tile[:, t, :] for tile in tiles])
+            return dst
+
+        def group(name):
+            return [sb("%s%d" % (name, j), [P, PACK, P]) for j in range(JT)]
+
+        def cols(tiles, j):
+            return tiles[j // 2][:, :, (j % 2) * P : (j % 2 + 1) * P]
+
+        m0, ta, tb, ts, u, shifted, d, td, v, resid, x = [
+            group(n) for n in ("m0_", "ta", "tb", "ts", "u", "shifted", "d", "td", "v", "resid", "x")
+        ]
+        tau = sb("tau", [P, PACK, S])
+        mag = sb("mag", [P, PACK, S])
+        num = sb("num", [P, PACK, S])
+        recip = [sb("recip%d" % t, [P, S]) for t in range(PACK)]
+        m1, trtT, fit, c = {}, {}, {}, {}
+
+        def outcomes(j):
+            acc0 = product(j, 0, "m0")
+            m1[j] = product(j, 1, "m1")
+            nc.scalar.copy(m0[j][:], acc0)
+
+        def propensity(j):
+            pe = product(j, 2, "pe_%d" % (j % 2))
+            nc.scalar.activation(ta[j][:], pe, ACT.Tanh, bias=-HALF_LN9, scale=-0.5)
+            nc.scalar.activation(tb[j][:], pe, ACT.Tanh, bias=HALF_LN9, scale=-0.5)
+            nc.scalar.activation(ts[j][:], pe, ACT.Tanh, scale=0.5)
+            nc.gpsimd.tensor_tensor(u[j][:], ta[j][:], tb[j][:], ALU.subtract)
+
+        def shift(j):
+            nc.gpsimd.tensor_scalar(shifted[j][:], ts[j][:], 1.0, 1.25, ALU.mult, ALU.add)
+
+        def turn_trt(j):
+            trtT[j] = turn("trt", "trtT%d" % j, [cols(trt_sb, j)])
+
+        def step_d(j):
+            nc.vector.tensor_tensor(d[j][:], m1[j], m0[j][:], ALU.subtract)
+
+        def step_td(j):
+            nc.vector.tensor_tensor(td[j][:], trtT[j][:], d[j][:], ALU.mult)
+            fit[j] = turn("fit", "fit%d" % j, [m0[j], td[j]])
+
+        def step_v(j):
+            nc.vector.scalar_tensor_tensor(v[j][:], u[j][:], 2.5, trtT[j][:], ALU.add, ALU.mult)
+            c[j] = turn("c", "c%d" % j, [tb[j], v[j]])
+
+        def step_resid(j):
+            nc.vector.tensor_tensor(resid[j][:], cols(yy_sb, j), fit[j][:], ALU.subtract)
+
+        def step_x(j):
+            nc.vector.scalar_tensor_tensor(x[j][:], c[j][:], -1.25, resid[j][:], ALU.add, ALU.mult)
+
+        def step_tau(j):
+            here = slice(j * P, (j + 1) * P)
+            dT = turn("dT" if j < 3 else "m0", "dT%d" % j, [d[j]])
+            nc.vector.scalar_tensor_tensor(tau[:, :, here], x[j][:], 4.0 / 3.0, dT[:], ALU.mult, ALU.add)
+
+        def magnitude(j):
+            here = slice(j * P, (j + 1) * P)
+            nc.scalar.activation(mag[:, :, here], tau[:, :, here], ACT.Abs)
+
+        def reciprocals(j, on_pool):
+            here = slice(j * P, (j + 1) * P)
+            root = keep.tile([P, PACK, P], F32, name="root%d" % j, tag="ta%d" % (JT - 1 - j), align_bytes=64)
+            nc.scalar.activation(root[:], mag[:, :, here], ACT.Abs_reciprocal_sqrt, bias=0.6)
+            for t in range(PACK):
+                if on_pool:
+                    nc.gpsimd.tensor_tensor(recip[t][:, here], root[:, t, :], root[:, t, :], ALU.mult)
+                else:
+                    nc.scalar.activation(recip[t][:, here], root[:, t, :], ACT.Square)
+
+        prop = {}
+
+        def turn_prop(t, tag):
+            prop[t] = bank(tag, [P, S], "prop%d" % t)
+            for j in range(JT):
+                turned_sum(prop[t][:, j * P : (j + 1) * P], [shifted[j][:, t, :]])
+
+        def step_num(here, t):
+            nc.vector.scalar_tensor_tensor(
+                num[:, t, here], prop[t][:, here], unit4[:, t : t + 1], tau[:, t, here], ALU.mult, ALU.mult
+            )
+
+        last = JT - 1
+        outcomes(0)
+        propensity(0)
+        turn_trt(0)
+        for j in range(JT):
+            if j + 1 < JT:
+                outcomes(j + 1)
+                propensity(j + 1)
+            step_d(j)
+            if j > 0:
+                step_resid(j - 1)
+            step_td(j)
+            if j > 0:
+                step_x(j - 1)
+            step_v(j)
+            if j + 1 < JT:
+                turn_trt(j + 1)
+            if j > 0:
+                step_tau(j - 1)
+                magnitude(j - 1)
+        step_resid(last)
+        step_x(last)
+        step_tau(last)
+        for j in range(last):
+            reciprocals(j, j < 2)
+        magnitude(last)
+        reciprocals(last, False)
+        for j in range(JT):
+            shift(j)
+        nc.gpsimd.tensor_scalar(unit4[:], unit_sb[:], 0.4, 0.0, ALU.mult, ALU.add)
+        for t, tag in enumerate(["pe_0","pe_1","m1","trt"]):
+            turn_prop(t, tag)
+        for h in range(2):
+            for t in range(PACK):
+                step_num(slice(h * HALF, (h + 1) * HALF), t)
+
+        twin = [tw_sb[:, 16 * h : 16 * h + 16] for h in range(2)]
+        fused = sb("fused", [P, PACK, HALF])
+        fetched = sb("fetched", [P, PACK, HALF])
+        for t in range(PACK):
+            nc.scalar.activation(fetched[:, t, :], recip[t][:].indirect(twin[1]), ACT.Copy)
+            nc.vector.tensor_tensor(fused[:, t, :], recip[t][:].indirect(twin[0]), num[:, t, 0:HALF], ALU.mult)
+
+        def woven(ap):
+            return ap.rearrange("p t (c i) -> p c t i", i=4)
+
+        out_v = out.rearrange("(a p) j -> p a j", p=P)
+        for n, (lo, hi, tag) in enumerate([(HALF, S, "fit"), (0, HALF, "c")]):
+            w = hi - lo
+            hid = sb("hid%d" % n, [P, w * PACK], BF16)
+            codes = sb("codes%d" % n, [P, w], U32)
+            planes = sb("planes%d" % n, [P, w], U8)
+            hid_v = hid[:].rearrange("p (c i t) -> p c t i", i=4, t=PACK)
+            if lo >= HALF:
+                nc.vector.tensor_tensor(hid_v, woven(fetched[:, :, lo - HALF : hi - HALF]), woven(num[:, :, lo:hi]), ALU.mult)
+            else:
+                nc.scalar.copy(hid_v, woven(fused[:, :, lo:hi]))
+            nc.vector.quantize_mx(out=codes[:].bitcast(FP8X4), scales=planes[:], in_=hid[:])
+            acc = bank(tag, [P, N // P, w], "out%d" % n)
+            for a in range(N // P):
+                nc.tensor.matmul_mx(
+                    out=acc[:, a, :],
+                    lhsT=w4w[:, 0, 2 * P * a : 2 * P * (a + 1)].bitcast(FP4X4),
+                    lhsT_scale=w4s[:, 0, P * a : P * (a + 1)],
+                    rhs=codes[:].bitcast(FP8X4),
+                    rhs_scale=planes[:],
+                    start=True,
+                    stop=True,
+                )
+            res = sb("res%d" % n, [P, N // P, w])
+            if n in (1,):
+                nc.vector.tensor_copy(res[:], acc[:])
+            else:
+                nc.scalar.copy(res[:], acc[:])
+            nc.sync.dma_start(out=out_v[:, :, lo:hi], in_=res[:])

@@ -21,9 +21,15 @@ ACT = mybir.ActivationFunctionType
 P = 128
 PACK = 4
 PASSES = K // (P * PACK)
-JT = S // P
+QUADRANTS = 4
+BLOCKS = S // P
+LAST = BLOCKS - 1
 HALF = S // 2
+PER_COLUMN = 16
 HALF_LN9 = 0.5 * math.log(9.0)
+ALL_PLANES = slice(0, PACK)
+PLANE_PAIRS = (slice(0, 2), slice(2, 4))
+BLOCKS_SQUARED_ON_GPSIMD = 2
 
 
 def tile_picked_yuplif_rel_p_kernel(
@@ -35,24 +41,14 @@ def tile_picked_yuplif_rel_p_kernel(
         keep = ctx.enter_context(tc.tile_pool(name="keep", bufs=1))
         psum = ctx.enter_context(tc.psum_pool(name="psum", bufs=1))
 
-        def sb(name, shape, dtype=F32):
-            return keep.tile(shape, dtype, name=name, tag=name, align_bytes=64)
+        def sb(name, shape, dtype=F32, tag=None):
+            return keep.tile(shape, dtype, name=name, tag=tag or name, align_bytes=64)
 
         def bank(tag, shape, name):
             return psum.tile(shape, F32, name=name, tag=tag)
 
-        def load_scales(queue, tile, scales, quadrants):
-            for q in quadrants:
-                queue.dma_start(
-                    out=tile[32 * q : 32 * q + 4, :, :].bitcast(I32),
-                    in_=scales[:, 4 * q : 4 * q + 4, :].rearrange("o r c -> r o c").bitcast(I32),
-                )
-
-        def load_fp4(queue, tile, words):
-            queue.dma_start(out=tile[:].bitcast(I32), in_=words.rearrange("o p c -> p o c").bitcast(I32))
-
-        offs_sb = keep.tile([P, S // 16], U16, name="offs_sb")
-        tw_sb = keep.tile([P, S // 16], U16, name="tw_sb")
+        offs_sb = keep.tile([P, S // PER_COLUMN], U16, name="offs_sb")
+        tw_sb = keep.tile([P, S // PER_COLUMN], U16, name="tw_sb")
         xw = [sb("xw%d" % o, [P, T], U32) for o in range(PASSES)]
         xs = sb("xs", [P, PASSES, T], U8)
         ww = [sb("ww%d" % a, [P, PASSES, 2 * H], U8) for a in range(3)]
@@ -60,60 +56,66 @@ def tile_picked_yuplif_rel_p_kernel(
         w4w = sb("w4w", [P, 1, 2 * N], U8)
         w4s = sb("w4s", [P, 1, N], U8)
         unit_sb = sb("unit_sb", [P, PACK])
-        unit4 = sb("unit4", [P, PACK])
+        unit_scaled = sb("unit_scaled", [P, PACK])
         trt_sb = [sb("trt%d" % h, [P, PACK, HALF]) for h in range(2)]
         yy_sb = [sb("yy%d" % h, [P, PACK, HALF]) for h in range(2)]
         ident = sb("ident", [P, P])
 
-        trt_v = trt.rearrange("(p t) j -> p t j", t=PACK)
-        yy_v = yy0.rearrange("(p t) j -> p t j", t=PACK)
+        def load_scale_rows(queue, tile, scales, q):
+            queue.dma_start(
+                out=tile[32 * q : 32 * q + 4, :, :].bitcast(I32),
+                in_=scales[:, 4 * q : 4 * q + 4, :].rearrange("o r c -> r o c").bitcast(I32),
+            )
 
-        def load_words(queue, o):
+        def load_fp4_words(queue, tile, words):
+            queue.dma_start(out=tile[:].bitcast(I32), in_=words.rearrange("o p c -> p o c").bitcast(I32))
+
+        def load_x_words(queue, o):
             queue.dma_start(out=xw[o][:].bitcast(I32), in_=x_words[o].rearrange("p n t -> p (n t)").bitcast(I32))
 
-        nc.vector.memset(xs[:].rearrange("p o c -> p (o c)").bitcast(I32), 0)
-        load_scales(nc.gpsimd, ws[0], w1_scales, (0, 1, 2, 3))
+        nc.gpsimd.memset(xs[:, 0, :].bitcast(I32), 0)
+        nc.vector.memset(xs[:, 1, :].bitcast(I32), 0)
+        for tile, words in zip(ww, (w1_words, w2_words, w3_words)):
+            load_fp4_words(nc.gpsimd, tile, words)
         make_identity(nc, ident[:])
         nc.sync.dma_start(offs_sb[:], offs)
-        load_scales(nc.sync, xs, x_scales, (0, 1, 2, 3))
-        load_words(nc.scalar, 0)
-        load_words(nc.scalar, 1)
-        load_fp4(nc.scalar, ww[0], w1_words)
-        load_fp4(nc.scalar, ww[1], w2_words)
-        load_fp4(nc.scalar, ww[2], w3_words)
-        nc.scalar.dma_start(out=trt_sb[0][:], in_=trt_v[:, :, 0:HALF])
-        load_scales(nc.sync, ws[1], w2_scales, (0, 1, 2, 3))
-        load_scales(nc.sync, ws[2], w3_scales, (0, 1, 2, 3))
-        nc.sync.dma_start(out=yy_sb[0][:], in_=yy_v[:, :, 0:HALF])
-        nc.sync.dma_start(out=trt_sb[1][:], in_=trt_v[:, :, HALF:S])
-        nc.sync.dma_start(out=yy_sb[1][:], in_=yy_v[:, :, HALF:S])
+        load_scale_rows(nc.scalar, ws[0], w1_scales, 0)
+        for q in range(0, QUADRANTS, 2):
+            load_scale_rows(nc.sync, xs, x_scales, q + 1)
+            load_scale_rows(nc.scalar, xs, x_scales, q)
+        load_x_words(nc.scalar, 0)
+        load_x_words(nc.sync, 1)
+        weight_rows = [(a, q) for a in range(3) for q in range(QUADRANTS)]
+        for a, q in weight_rows[1:]:
+            on_sync = q % 2 == 1 and (a, q) != weight_rows[-1]
+            load_scale_rows(nc.sync if on_sync else nc.scalar, ws[a], (w1_scales, w2_scales, w3_scales)[a], q)
+        trt_v = trt.rearrange("(p t) j -> p t j", t=PACK)
+        yy_v = yy0.rearrange("(p t) j -> p t j", t=PACK)
+        for h in range(2):
+            nc.sync.dma_start(out=trt_sb[h][:], in_=trt_v[:, :, h * HALF : (h + 1) * HALF])
+            nc.sync.dma_start(out=yy_sb[h][:], in_=yy_v[:, :, h * HALF : (h + 1) * HALF])
         nc.sync.dma_start(out=unit_sb[:], in_=unit.rearrange("(p t) o -> p (t o)", t=PACK))
         nc.sync.dma_start(tw_sb[:], tw)
-        load_fp4(nc.sync, w4w, w4_words)
-        load_scales(nc.sync, w4s, w4_scales, (0, 1, 2, 3))
+        load_fp4_words(nc.sync, w4w, w4_words)
+        for q in range(QUADRANTS):
+            load_scale_rows(nc.sync, w4s, w4_scales, q)
 
         gw = [sb("gw%d" % o, [P, S], U32) for o in range(PASSES)]
         gs = [sb("gs%d" % o, [P, S], U8) for o in range(PASSES)]
-
-        def pick_words(o, lo, hi):
-            nc.vector.tensor_copy(gw[o][:, lo:hi], xw[o][:].indirect(offs_sb[:, lo // 16 : hi // 16]))
-
-        def pick_scales(lo, hi):
+        for o in range(PASSES):
+            nc.vector.tensor_copy(gs[o][:], xs[:, o, :].indirect(offs_sb[:]))
+        for lo, hi in ((0, P), (P, S)):
             for o in range(PASSES):
-                nc.vector.tensor_copy(gs[o][:, lo:hi], xs[:, o, :].indirect(offs_sb[:, lo // 16 : hi // 16]))
+                entries = offs_sb[:, lo // PER_COLUMN : hi // PER_COLUMN]
+                nc.vector.tensor_copy(gw[o][:, lo:hi], xw[o][:].indirect(entries))
 
-        pick_words(0, 0, S)
-        pick_words(1, 0, S)
-        pick_scales(0, P)
-        pick_scales(P, S)
-
-        def product(j, a, tag):
-            acc = bank(tag, [P, H], "acc%d_%d" % (a, j))
+        def product(b, a, tag):
+            acc = bank(tag, [P, H], "acc%d_%d" % (a, b))
             for o in range(PASSES):
                 nc.tensor.matmul_mx(
                     out=acc[:],
-                    lhsT=gw[o][:, j * P : (j + 1) * P].bitcast(FP8X4),
-                    lhsT_scale=gs[o][:, j * P : (j + 1) * P],
+                    lhsT=gw[o][:, b * P : (b + 1) * P].bitcast(FP8X4),
+                    lhsT_scale=gs[o][:, b * P : (b + 1) * P],
                     rhs=ww[a][:, o, :].bitcast(FP4X4),
                     rhs_scale=ws[a][:, o, :],
                     start=(o == 0),
@@ -131,124 +133,123 @@ def tile_picked_yuplif_rel_p_kernel(
                 turned_sum(dst[:, t, :], [tile[:, t, :] for tile in tiles])
             return dst
 
-        def group(name):
-            return [sb("%s%d" % (name, j), [P, PACK, P]) for j in range(JT)]
+        def per_block(name):
+            return [sb("%s%d" % (name, b), [P, PACK, P]) for b in range(BLOCKS)]
 
-        def cols(tiles, j):
-            return tiles[j // 2][:, :, (j % 2) * P : (j % 2 + 1) * P]
+        def block_of_halves(tiles, b):
+            return tiles[b // 2][:, :, (b % 2) * P : (b % 2 + 1) * P]
+
+        def columns(b):
+            return slice(b * P, (b + 1) * P)
 
         m0, ta, tb, ts, u, shifted, d, td, v, resid, x = [
-            group(n) for n in ("m0_", "ta", "tb", "ts", "u", "shifted", "d", "td", "v", "resid", "x")
+            per_block(name) for name in ("m0_", "ta", "tb", "ts", "u", "shifted", "d", "td", "v", "resid", "x")
         ]
         tau = sb("tau", [P, PACK, S])
         mag = sb("mag", [P, PACK, S])
         num = sb("num", [P, PACK, S])
         recip = [sb("recip%d" % t, [P, S]) for t in range(PACK)]
-        m1, trtT, fit, c = {}, {}, {}, {}
+        m1, trt_turned, fit, c, d_turned, root = {}, {}, {}, {}, {}, {}
 
-        def outcomes(j):
-            acc0 = product(j, 0, "m0")
-            m1[j] = product(j, 1, "m1")
-            nc.scalar.copy(m0[j][:], acc0)
+        def outcomes(b):
+            acc0 = product(b, 0, "m0")
+            m1[b] = product(b, 1, "m1")
+            nc.scalar.copy(m0[b][:], acc0)
 
-        def propensity(j):
-            pe = product(j, 2, "pe_%d" % (j % 2))
-            nc.scalar.activation(ta[j][:], pe, ACT.Tanh, bias=-HALF_LN9, scale=-0.5)
-            nc.scalar.activation(tb[j][:], pe, ACT.Tanh, bias=HALF_LN9, scale=-0.5)
-            nc.scalar.activation(ts[j][:], pe, ACT.Tanh, scale=0.5)
-            nc.gpsimd.tensor_tensor(u[j][:], ta[j][:], tb[j][:], ALU.subtract)
+        def propensity(b):
+            pe = product(b, 2, "pe_%d" % (b % 2))
+            nc.scalar.activation(ta[b][:], pe, ACT.Tanh, bias=-HALF_LN9, scale=-0.5)
+            nc.scalar.activation(tb[b][:], pe, ACT.Tanh, bias=HALF_LN9, scale=-0.5)
+            nc.scalar.activation(ts[b][:], pe, ACT.Tanh, scale=0.5)
+            engine = nc.vector if b == 0 else nc.gpsimd
+            engine.tensor_tensor(u[b][:], ta[b][:], tb[b][:], ALU.subtract)
 
-        def shift(j):
-            nc.gpsimd.tensor_scalar(shifted[j][:], ts[j][:], 1.0, 1.25, ALU.mult, ALU.add)
+        def turn_trt(b):
+            trt_turned[b] = turn("trt", "trt_turned%d" % b, [block_of_halves(trt_sb, b)])
 
-        def turn_trt(j):
-            trtT[j] = turn("trt", "trtT%d" % j, [cols(trt_sb, j)])
+        def turn_d(b):
+            d_turned[b] = turn(("dT", "dT", "pe_0", "m0")[b], "d_turned%d" % b, [d[b]])
 
-        def step_d(j):
-            nc.vector.tensor_tensor(d[j][:], m1[j], m0[j][:], ALU.subtract)
+        def step_resid(b):
+            nc.vector.tensor_tensor(resid[b][:], block_of_halves(yy_sb, b), fit[b][:], ALU.subtract)
 
-        def step_td(j):
-            nc.vector.tensor_tensor(td[j][:], trtT[j][:], d[j][:], ALU.mult)
-            fit[j] = turn("fit", "fit%d" % j, [m0[j], td[j]])
-
-        def step_v(j):
-            nc.vector.scalar_tensor_tensor(v[j][:], u[j][:], 2.5, trtT[j][:], ALU.add, ALU.mult)
-            c[j] = turn("c", "c%d" % j, [tb[j], v[j]])
-
-        def step_resid(j):
-            nc.vector.tensor_tensor(resid[j][:], cols(yy_sb, j), fit[j][:], ALU.subtract)
-
-        def step_x(j):
-            nc.vector.scalar_tensor_tensor(x[j][:], c[j][:], -1.25, resid[j][:], ALU.add, ALU.mult)
-
-        def step_tau(j):
-            here = slice(j * P, (j + 1) * P)
-            dT = turn("dT" if j < 3 else "m0", "dT%d" % j, [d[j]])
-            nc.vector.scalar_tensor_tensor(tau[:, :, here], x[j][:], 4.0 / 3.0, dT[:], ALU.mult, ALU.add)
-
-        def magnitude(j):
-            here = slice(j * P, (j + 1) * P)
-            nc.scalar.activation(mag[:, :, here], tau[:, :, here], ACT.Abs)
-
-        def reciprocals(j, on_pool):
-            here = slice(j * P, (j + 1) * P)
-            root = keep.tile([P, PACK, P], F32, name="root%d" % j, tag="ta%d" % (JT - 1 - j), align_bytes=64)
-            nc.scalar.activation(root[:], mag[:, :, here], ACT.Abs_reciprocal_sqrt, bias=0.6)
-            for t in range(PACK):
-                if on_pool:
-                    nc.gpsimd.tensor_tensor(recip[t][:, here], root[:, t, :], root[:, t, :], ALU.mult)
-                else:
-                    nc.scalar.activation(recip[t][:, here], root[:, t, :], ACT.Square)
-
-        prop = {}
-
-        def turn_prop(t, tag):
-            prop[t] = bank(tag, [P, S], "prop%d" % t)
-            for j in range(JT):
-                turned_sum(prop[t][:, j * P : (j + 1) * P], [shifted[j][:, t, :]])
-
-        def step_num(here, t):
+        def step_x(b, planes):
             nc.vector.scalar_tensor_tensor(
-                num[:, t, here], prop[t][:, here], unit4[:, t : t + 1], tau[:, t, here], ALU.mult, ALU.mult
+                x[b][:, planes, :], c[b][:, planes, :], -1.25, resid[b][:, planes, :], ALU.add, ALU.mult
             )
 
-        last = JT - 1
+        def step_tau(b, planes):
+            nc.vector.scalar_tensor_tensor(
+                tau[:, planes, columns(b)], x[b][:, planes, :], 4.0 / 3.0, d_turned[b][:, planes, :], ALU.mult, ALU.add
+            )
+
+        def magnitude(b, planes):
+            nc.scalar.activation(mag[:, planes, columns(b)], tau[:, planes, columns(b)], ACT.Abs)
+
+        def reciprocals(b, planes):
+            nc.scalar.activation(root[b][:, planes, :], mag[:, planes, columns(b)], ACT.Abs_reciprocal_sqrt, bias=0.6)
+            for t in range(planes.start, planes.stop):
+                if b < BLOCKS_SQUARED_ON_GPSIMD:
+                    nc.gpsimd.tensor_tensor(recip[t][:, columns(b)], root[b][:, t, :], root[b][:, t, :], ALU.mult)
+                else:
+                    nc.scalar.activation(recip[t][:, columns(b)], root[b][:, t, :], ACT.Square)
+
         outcomes(0)
         propensity(0)
         turn_trt(0)
-        for j in range(JT):
-            if j + 1 < JT:
-                outcomes(j + 1)
-                propensity(j + 1)
-            step_d(j)
-            if j > 0:
-                step_resid(j - 1)
-            step_td(j)
-            if j > 0:
-                step_x(j - 1)
-            step_v(j)
-            if j + 1 < JT:
-                turn_trt(j + 1)
-            if j > 0:
-                step_tau(j - 1)
-                magnitude(j - 1)
-        step_resid(last)
-        step_x(last)
-        step_tau(last)
-        for j in range(last):
-            reciprocals(j, j < 2)
-        magnitude(last)
-        reciprocals(last, False)
-        for j in range(JT):
-            shift(j)
-        nc.gpsimd.tensor_scalar(unit4[:], unit_sb[:], 0.4, 0.0, ALU.mult, ALU.add)
-        for t, tag in enumerate(["pe_0","pe_1","m1","trt"]):
-            turn_prop(t, tag)
-        for h in range(2):
-            for t in range(PACK):
-                step_num(slice(h * HALF, (h + 1) * HALF), t)
+        propensity(1)
+        for b in range(BLOCKS):
+            if b + 1 < BLOCKS:
+                outcomes(b + 1)
+            if b + 2 < BLOCKS:
+                propensity(b + 2)
+            nc.vector.tensor_tensor(d[b][:], m1[b], m0[b][:], ALU.subtract)
+            if b > 0:
+                step_resid(b - 1)
+            nc.vector.tensor_tensor(td[b][:], trt_turned[b][:], d[b][:], ALU.mult)
+            fit[b] = turn("fit", "fit%d" % b, [m0[b], td[b]])
+            if b > 0:
+                step_x(b - 1, ALL_PLANES)
+            nc.vector.scalar_tensor_tensor(v[b][:], u[b][:], 2.5, trt_turned[b][:], ALU.add, ALU.mult)
+            if b + 1 < BLOCKS:
+                turn_trt(b + 1)
+            if b >= 2:
+                turn_d(b)
+            c[b] = turn("c", "c%d" % b, [tb[b], v[b]])
+            if b > 0:
+                if b - 1 < 2:
+                    turn_d(b - 1)
+                step_tau(b - 1, ALL_PLANES)
+                magnitude(b - 1, ALL_PLANES)
 
-        twin = [tw_sb[:, 16 * h : 16 * h + 16] for h in range(2)]
+        step_resid(LAST)
+        for planes in PLANE_PAIRS:
+            step_x(LAST, planes)
+        for planes in PLANE_PAIRS:
+            step_tau(LAST, planes)
+        for b in range(BLOCKS):
+            root[b] = sb("root%d" % b, [P, PACK, P], tag="ta%d" % (LAST - b))
+            if b < LAST:
+                reciprocals(b, ALL_PLANES)
+        for planes in PLANE_PAIRS:
+            magnitude(LAST, planes)
+            reciprocals(LAST, planes)
+
+        for b in range(BLOCKS):
+            nc.gpsimd.tensor_scalar(shifted[b][:], ts[b][:], 1.0, 1.25, ALU.mult, ALU.add)
+        nc.gpsimd.tensor_scalar(unit_scaled[:], unit_sb[:], 0.4, 0.0, ALU.mult, ALU.add)
+        shifted_turned = []
+        for t, tag in enumerate(("pe_1", "m1", "dT", "trt")):
+            dst = bank(tag, [P, S], "shifted_turned%d" % t)
+            for b in range(BLOCKS):
+                turned_sum(dst[:, columns(b)], [shifted[b][:, t, :]])
+            shifted_turned.append(dst)
+        for t in range(PACK):
+            nc.vector.scalar_tensor_tensor(
+                num[:, t, :], shifted_turned[t][:], unit_scaled[:, t : t + 1], tau[:, t, :], ALU.mult, ALU.mult
+            )
+
+        twin = [tw_sb[:, h * HALF // PER_COLUMN : (h + 1) * HALF // PER_COLUMN] for h in range(2)]
         fused = sb("fused", [P, PACK, HALF])
         fetched = sb("fetched", [P, PACK, HALF])
         for t in range(PACK):
@@ -256,34 +257,34 @@ def tile_picked_yuplif_rel_p_kernel(
             nc.vector.tensor_tensor(fused[:, t, :], recip[t][:].indirect(twin[0]), num[:, t, 0:HALF], ALU.mult)
 
         def woven(ap):
-            return ap.rearrange("p t (c i) -> p c t i", i=4)
+            return ap.rearrange("p t (g i) -> p g t i", i=4)
 
         out_v = out.rearrange("(a p) j -> p a j", p=P)
-        for n, (lo, hi, tag) in enumerate([(HALF, S, "fit"), (0, HALF, "c")]):
-            w = hi - lo
-            hid = sb("hid%d" % n, [P, w * PACK], BF16)
-            codes = sb("codes%d" % n, [P, w], U32)
-            planes = sb("planes%d" % n, [P, w], U8)
-            hid_v = hid[:].rearrange("p (c i t) -> p c t i", i=4, t=PACK)
-            if lo >= HALF:
-                nc.vector.tensor_tensor(hid_v, woven(fetched[:, :, lo - HALF : hi - HALF]), woven(num[:, :, lo:hi]), ALU.mult)
+        for n, (b, tag) in enumerate(zip((2, 0, 3, 1), ("fit", "c", "dT", "m0"))):
+            hid = sb("hid%d" % n, [P, P * PACK], BF16)
+            codes = sb("codes%d" % n, [P, P], U32)
+            code_scales = sb("code_scales%d" % n, [P, P], U8)
+            hid_v = hid[:].rearrange("p (g i t) -> p g t i", i=4, t=PACK)
+            if b >= BLOCKS // 2:
+                twins = woven(fetched[:, :, columns(b - BLOCKS // 2)])
+                nc.vector.tensor_tensor(hid_v, twins, woven(num[:, :, columns(b)]), ALU.mult)
             else:
-                nc.scalar.copy(hid_v, woven(fused[:, :, lo:hi]))
-            nc.vector.quantize_mx(out=codes[:].bitcast(FP8X4), scales=planes[:], in_=hid[:])
-            acc = bank(tag, [P, N // P, w], "out%d" % n)
+                nc.scalar.copy(hid_v, woven(fused[:, :, columns(b)]))
+            nc.vector.quantize_mx(out=codes[:].bitcast(FP8X4), scales=code_scales[:], in_=hid[:])
+            acc = bank(tag, [P, N // P, P], "out%d" % n)
             for a in range(N // P):
                 nc.tensor.matmul_mx(
                     out=acc[:, a, :],
                     lhsT=w4w[:, 0, 2 * P * a : 2 * P * (a + 1)].bitcast(FP4X4),
                     lhsT_scale=w4s[:, 0, P * a : P * (a + 1)],
                     rhs=codes[:].bitcast(FP8X4),
-                    rhs_scale=planes[:],
+                    rhs_scale=code_scales[:],
                     start=True,
                     stop=True,
                 )
-            res = sb("res%d" % n, [P, N // P, w])
-            if n in (1,):
-                nc.vector.tensor_copy(res[:], acc[:])
-            else:
+            res = sb("res%d" % n, [P, N // P, P])
+            if n % 2 == 0:
                 nc.scalar.copy(res[:], acc[:])
-            nc.sync.dma_start(out=out_v[:, :, lo:hi], in_=res[:])
+            else:
+                nc.vector.tensor_copy(res[:], acc[:])
+            nc.sync.dma_start(out=out_v[:, :, columns(b)], in_=res[:])

import math
from contextlib import ExitStack

import concourse.mybir as mybir
from concourse.masks import make_identity

K, T, S, N, H = 1024, 1024, 512, 256, 512
FLOPS = 2 * (3 * K * H * S + H * N * S)

F32 = mybir.dt.float32
BF16 = mybir.dt.bfloat16
I32 = mybir.dt.int32
U32 = mybir.dt.uint32
U16 = mybir.dt.uint16
U8 = mybir.dt.uint8
FP8X4 = mybir.dt.float8_e4m3fn_x4
FP4X4 = mybir.dt.float4_e2m1fn_x4
ALU = mybir.AluOpType
ACT = mybir.ActivationFunctionType

P = 128
PACK = 4
PASSES = K // (P * PACK)
QUADRANTS = 4
BLOCKS = S // P
LAST = BLOCKS - 1
HALF = S // 2
PER_COLUMN = 16
HALF_LN9 = 0.5 * math.log(9.0)
ALL_PLANES = slice(0, PACK)
PLANE_PAIRS = (slice(0, 2), slice(2, 4))
BLOCKS_SQUARED_ON_GPSIMD = 2


def tile_picked_yuplif_rel_p_kernel(
    tc, x_words, x_scales, w1_words, w1_scales, w2_words, w2_scales, w3_words, w3_scales,
    trt, yy0, unit, w4_words, w4_scales, offs, tw, out,
):
    nc = tc.nc
    with ExitStack() as ctx:
        keep = ctx.enter_context(tc.tile_pool(name="keep", bufs=1))
        psum = ctx.enter_context(tc.psum_pool(name="psum", bufs=1))

        def sb(name, shape, dtype=F32, tag=None):
            return keep.tile(shape, dtype, name=name, tag=tag or name, align_bytes=64)

        def bank(tag, shape, name):
            return psum.tile(shape, F32, name=name, tag=tag)

        offs_sb = keep.tile([P, S // PER_COLUMN], U16, name="offs_sb")
        tw_sb = keep.tile([P, S // PER_COLUMN], U16, name="tw_sb")
        xw = [sb("xw%d" % o, [P, T], U32) for o in range(PASSES)]
        xs = sb("xs", [P, PASSES, T], U8)
        ww = [sb("ww%d" % a, [P, PASSES, 2 * H], U8) for a in range(3)]
        ws = [sb("ws%d" % a, [P, PASSES, H], U8) for a in range(3)]
        w4w = sb("w4w", [P, 1, 2 * N], U8)
        w4s = sb("w4s", [P, 1, N], U8)
        unit_sb = sb("unit_sb", [P, PACK])
        unit_scaled = sb("unit_scaled", [P, PACK])
        trt_sb = [sb("trt%d" % h, [P, PACK, HALF]) for h in range(2)]
        yy_sb = [sb("yy%d" % h, [P, PACK, HALF]) for h in range(2)]
        ident = sb("ident", [P, P])

        def load_scale_rows(queue, tile, scales, q):
            queue.dma_start(
                out=tile[32 * q : 32 * q + 4, :, :].bitcast(I32),
                in_=scales[:, 4 * q : 4 * q + 4, :].rearrange("o r c -> r o c").bitcast(I32),
            )

        def load_fp4_words(queue, tile, words):
            queue.dma_start(out=tile[:].bitcast(I32), in_=words.rearrange("o p c -> p o c").bitcast(I32))

        def load_x_words(queue, o):
            queue.dma_start(out=xw[o][:].bitcast(I32), in_=x_words[o].rearrange("p n t -> p (n t)").bitcast(I32))

        nc.gpsimd.memset(xs[:, 0, :].bitcast(I32), 0)
        nc.vector.memset(xs[:, 1, :].bitcast(I32), 0)
        for tile, words in zip(ww, (w1_words, w2_words, w3_words)):
            load_fp4_words(nc.gpsimd, tile, words)
        make_identity(nc, ident[:])
        nc.sync.dma_start(offs_sb[:], offs)
        load_scale_rows(nc.scalar, ws[0], w1_scales, 0)
        for q in range(0, QUADRANTS, 2):
            load_scale_rows(nc.sync, xs, x_scales, q + 1)
            load_scale_rows(nc.scalar, xs, x_scales, q)
        load_x_words(nc.scalar, 0)
        load_x_words(nc.sync, 1)
        weight_rows = [(a, q) for a in range(3) for q in range(QUADRANTS)]
        for a, q in weight_rows[1:]:
            on_sync = q % 2 == 1 and (a, q) != weight_rows[-1]
            load_scale_rows(nc.sync if on_sync else nc.scalar, ws[a], (w1_scales, w2_scales, w3_scales)[a], q)
        trt_v = trt.rearrange("(p t) j -> p t j", t=PACK)
        yy_v = yy0.rearrange("(p t) j -> p t j", t=PACK)
        for h in range(2):
            nc.sync.dma_start(out=trt_sb[h][:], in_=trt_v[:, :, h * HALF : (h + 1) * HALF])
            nc.sync.dma_start(out=yy_sb[h][:], in_=yy_v[:, :, h * HALF : (h + 1) * HALF])
        nc.sync.dma_start(out=unit_sb[:], in_=unit.rearrange("(p t) o -> p (t o)", t=PACK))
        nc.sync.dma_start(tw_sb[:], tw)
        load_fp4_words(nc.sync, w4w, w4_words)
        for q in range(QUADRANTS):
            load_scale_rows(nc.sync, w4s, w4_scales, q)

        gw = [sb("gw%d" % o, [P, S], U32) for o in range(PASSES)]
        gs = [sb("gs%d" % o, [P, S], U8) for o in range(PASSES)]
        for o in range(PASSES):
            nc.vector.tensor_copy(gs[o][:], xs[:, o, :].indirect(offs_sb[:]))
        for lo, hi in ((0, P), (P, S)):
            for o in range(PASSES):
                entries = offs_sb[:, lo // PER_COLUMN : hi // PER_COLUMN]
                nc.vector.tensor_copy(gw[o][:, lo:hi], xw[o][:].indirect(entries))

        def product(b, a, tag):
            acc = bank(tag, [P, H], "acc%d_%d" % (a, b))
            for o in range(PASSES):
                nc.tensor.matmul_mx(
                    out=acc[:],
                    lhsT=gw[o][:, b * P : (b + 1) * P].bitcast(FP8X4),
                    lhsT_scale=gs[o][:, b * P : (b + 1) * P],
                    rhs=ww[a][:, o, :].bitcast(FP4X4),
                    rhs_scale=ws[a][:, o, :],
                    start=(o == 0),
                    stop=(o == PASSES - 1),
                )
            return acc[:].rearrange("p (m t) -> p t m", t=PACK)

        def turned_sum(dst, terms):
            for n, term in enumerate(terms):
                nc.tensor.matmul(dst, term, ident[:], start=(n == 0), stop=(n == len(terms) - 1), is_transpose=True)

        def turn(tag, name, tiles):
            dst = bank(tag, [P, PACK, P], name)
            for t in range(PACK):
                turned_sum(dst[:, t, :], [tile[:, t, :] for tile in tiles])
            return dst

        def per_block(name):
            return [sb("%s%d" % (name, b), [P, PACK, P]) for b in range(BLOCKS)]

        def block_of_halves(tiles, b):
            return tiles[b // 2][:, :, (b % 2) * P : (b % 2 + 1) * P]

        def columns(b):
            return slice(b * P, (b + 1) * P)

        m0, ta, tb, ts, u, shifted, d, td, v, resid, x = [
            per_block(name) for name in ("m0_", "ta", "tb", "ts", "u", "shifted", "d", "td", "v", "resid", "x")
        ]
        tau = sb("tau", [P, PACK, S])
        mag = sb("mag", [P, PACK, S])
        num = sb("num", [P, PACK, S])
        recip = [sb("recip%d" % t, [P, S]) for t in range(PACK)]
        m1, trt_turned, fit, c, d_turned, root = {}, {}, {}, {}, {}, {}

        def outcomes(b):
            acc0 = product(b, 0, "m0")
            m1[b] = product(b, 1, "m1")
            nc.scalar.copy(m0[b][:], acc0)

        def propensity(b):
            pe = product(b, 2, "pe_%d" % (b % 2))
            nc.scalar.activation(ta[b][:], pe, ACT.Tanh, bias=-HALF_LN9, scale=-0.5)
            nc.scalar.activation(tb[b][:], pe, ACT.Tanh, bias=HALF_LN9, scale=-0.5)
            nc.scalar.activation(ts[b][:], pe, ACT.Tanh, scale=0.5)
            engine = nc.vector if b == 0 else nc.gpsimd
            engine.tensor_tensor(u[b][:], ta[b][:], tb[b][:], ALU.subtract)

        def turn_trt(b):
            trt_turned[b] = turn("trt", "trt_turned%d" % b, [block_of_halves(trt_sb, b)])

        def turn_d(b):
            d_turned[b] = turn(("dT", "dT", "pe_0", "m0")[b], "d_turned%d" % b, [d[b]])

        def step_resid(b):
            nc.vector.tensor_tensor(resid[b][:], block_of_halves(yy_sb, b), fit[b][:], ALU.subtract)

        def step_x(b, planes):
            nc.vector.scalar_tensor_tensor(
                x[b][:, planes, :], c[b][:, planes, :], -1.25, resid[b][:, planes, :], ALU.add, ALU.mult
            )

        def step_tau(b, planes):
            nc.vector.scalar_tensor_tensor(
                tau[:, planes, columns(b)], x[b][:, planes, :], 4.0 / 3.0, d_turned[b][:, planes, :], ALU.mult, ALU.add
            )

        def magnitude(b, planes):
            nc.scalar.activation(mag[:, planes, columns(b)], tau[:, planes, columns(b)], ACT.Abs)

        def reciprocals(b, planes):
            nc.scalar.activation(root[b][:, planes, :], mag[:, planes, columns(b)], ACT.Abs_reciprocal_sqrt, bias=0.6)
            for t in range(planes.start, planes.stop):
                if b < BLOCKS_SQUARED_ON_GPSIMD:
                    nc.gpsimd.tensor_tensor(recip[t][:, columns(b)], root[b][:, t, :], root[b][:, t, :], ALU.mult)
                else:
                    nc.scalar.activation(recip[t][:, columns(b)], root[b][:, t, :], ACT.Square)

        outcomes(0)
        propensity(0)
        turn_trt(0)
        propensity(1)
        for b in range(BLOCKS):
            if b + 1 < BLOCKS:
                outcomes(b + 1)
            if b + 2 < BLOCKS:
                propensity(b + 2)
            nc.vector.tensor_tensor(d[b][:], m1[b], m0[b][:], ALU.subtract)
            if b > 0:
                step_resid(b - 1)
            nc.vector.tensor_tensor(td[b][:], trt_turned[b][:], d[b][:], ALU.mult)
            fit[b] = turn("fit", "fit%d" % b, [m0[b], td[b]])
            if b > 0:
                step_x(b - 1, ALL_PLANES)
            nc.vector.scalar_tensor_tensor(v[b][:], u[b][:], 2.5, trt_turned[b][:], ALU.add, ALU.mult)
            if b + 1 < BLOCKS:
                turn_trt(b + 1)
            if b >= 2:
                turn_d(b)
            c[b] = turn("c", "c%d" % b, [tb[b], v[b]])
            if b > 0:
                if b - 1 < 2:
                    turn_d(b - 1)
                step_tau(b - 1, ALL_PLANES)
                magnitude(b - 1, ALL_PLANES)

        step_resid(LAST)
        for planes in PLANE_PAIRS:
            step_x(LAST, planes)
        for planes in PLANE_PAIRS:
            step_tau(LAST, planes)
        for b in range(BLOCKS):
            root[b] = sb("root%d" % b, [P, PACK, P], tag="ta%d" % (LAST - b))
            if b < LAST:
                reciprocals(b, ALL_PLANES)
        for planes in PLANE_PAIRS:
            magnitude(LAST, planes)
            reciprocals(LAST, planes)

        for b in range(BLOCKS):
            nc.gpsimd.tensor_scalar(shifted[b][:], ts[b][:], 1.0, 1.25, ALU.mult, ALU.add)
        nc.gpsimd.tensor_scalar(unit_scaled[:], unit_sb[:], 0.4, 0.0, ALU.mult, ALU.add)
        shifted_turned = []
        for t, tag in enumerate(("pe_1", "m1", "dT", "trt")):
            dst = bank(tag, [P, S], "shifted_turned%d" % t)
            for b in range(BLOCKS):
                turned_sum(dst[:, columns(b)], [shifted[b][:, t, :]])
            shifted_turned.append(dst)
        for t in range(PACK):
            nc.vector.scalar_tensor_tensor(
                num[:, t, :], shifted_turned[t][:], unit_scaled[:, t : t + 1], tau[:, t, :], ALU.mult, ALU.mult
            )

        twin = [tw_sb[:, h * HALF // PER_COLUMN : (h + 1) * HALF // PER_COLUMN] for h in range(2)]
        fused = sb("fused", [P, PACK, HALF])
        fetched = sb("fetched", [P, PACK, HALF])
        for t in range(PACK):
            nc.scalar.activation(fetched[:, t, :], recip[t][:].indirect(twin[1]), ACT.Copy)
            nc.vector.tensor_tensor(fused[:, t, :], recip[t][:].indirect(twin[0]), num[:, t, 0:HALF], ALU.mult)

        def woven(ap):
            return ap.rearrange("p t (g i) -> p g t i", i=4)

        out_v = out.rearrange("(a p) j -> p a j", p=P)
        for n, (b, tag) in enumerate(zip((2, 0, 3, 1), ("fit", "c", "dT", "m0"))):
            hid = sb("hid%d" % n, [P, P * PACK], BF16)
            codes = sb("codes%d" % n, [P, P], U32)
            code_scales = sb("code_scales%d" % n, [P, P], U8)
            hid_v = hid[:].rearrange("p (g i t) -> p g t i", i=4, t=PACK)
            if b >= BLOCKS // 2:
                twins = woven(fetched[:, :, columns(b - BLOCKS // 2)])
                nc.vector.tensor_tensor(hid_v, twins, woven(num[:, :, columns(b)]), ALU.mult)
            else:
                nc.scalar.copy(hid_v, woven(fused[:, :, columns(b)]))
            nc.vector.quantize_mx(out=codes[:].bitcast(FP8X4), scales=code_scales[:], in_=hid[:])
            acc = bank(tag, [P, N // P, P], "out%d" % n)
            for a in range(N // P):
                nc.tensor.matmul_mx(
                    out=acc[:, a, :],
                    lhsT=w4w[:, 0, 2 * P * a : 2 * P * (a + 1)].bitcast(FP4X4),
                    lhsT_scale=w4s[:, 0, P * a : P * (a + 1)],
                    rhs=codes[:].bitcast(FP8X4),
                    rhs_scale=code_scales[:],
                    start=True,
                    stop=True,
                )
            res = sb("res%d" % n, [P, N // P, P])
            if n % 2 == 0:
                nc.scalar.copy(res[:], acc[:])
            else:
                nc.vector.tensor_copy(res[:], acc[:])
            nc.sync.dma_start(out=out_v[:, :, columns(b)], in_=res[:])
